import numpy as np
import ml_dtypes


def mxq(x, axis, fmt="e4m3"):
    dtype, down = {"e4m3": (ml_dtypes.float8_e4m3fn, 7), "e5m2": (ml_dtypes.float8_e5m2, 14)}[fmt]
    v = np.moveaxis(np.asarray(x, np.float32).astype(ml_dtypes.bfloat16).astype(np.float64), axis, -1)
    blocks = v.reshape(v.shape[:-1] + (-1, 32))
    amax = np.abs(blocks).max(-1, keepdims=True)
    byte = np.maximum(np.where(amax > 0, np.frexp(amax)[1] - 1 + 127, 0) - down, 1)
    scale = np.exp2(byte - 127.0)
    codes = (blocks / scale).astype(np.float32).astype(dtype).astype(np.float64)
    return np.moveaxis((codes * scale).reshape(v.shape), -1, axis)


WIDE = False


def mx_kscale(k):
    if not WIDE:
        return np.ones(k)
    levels = np.array([10, -10, 5, -5, 0])
    if k % 512:
        return np.exp2(np.random.permutation(np.resize(levels, k // 32))).repeat(32)
    a = np.empty((k // 512, 16))
    for p in range(k // 512):
        a[p, :8] = np.random.permutation(np.resize(levels, 8))
        for g in range(8):
            far = levels[np.abs(levels - a[p, g]) >= 10]
            a[p, g + 8] = far[np.random.randint(len(far))]
    return np.exp2(a.ravel()).repeat(32)


def f64(x):
    return np.asarray(x).astype(np.float64)


def striped(idx):
    return np.tile(idx.reshape(-1, 16).T, (8, 1)).astype(np.uint16)


def unstriped(offs):
    return offs[:16].T.reshape(-1).astype(np.int64)


def pack_weight(w):
    k, n = w.shape
    w = f64(np.asarray(w, np.float32).astype(ml_dtypes.bfloat16)).reshape(k // 32, 32, n)
    amax = np.abs(w).max(1)
    byte = np.clip(np.where(amax > 0, np.frexp(amax)[1] - 1 + 127 - 7, 1), 1, 254)
    scaled = (w * np.exp2(127.0 - byte)[:, None, :]).reshape(k, n).astype(np.float32)
    words = np.ascontiguousarray(scaled.reshape(k // 512, 128, 4, n).transpose(0, 1, 3, 2)).astype(ml_dtypes.float8_e4m3fn).view(np.uint8)
    return words, np.ascontiguousarray(byte.astype(np.uint8).reshape(k // 512, 16, n))


def unpack_weight(words, scales):
    g, p, n, _ = words.shape
    vals = np.ascontiguousarray(words).view(ml_dtypes.float8_e4m3fn).astype(np.float64) * np.repeat(np.exp2(scales.astype(np.float64) - 127.0), 8, axis=1)[..., None]
    return vals.transpose(0, 1, 3, 2).reshape(g * 512, n)


def relu(v):
    return np.maximum(v, 0.0)


K, T, S, H, N, D, U, W = 512, 1024, 512, 512, 128, 4, 512, 1024


def setup_inputs():
    n = np.random.standard_normal
    s = mx_kscale(K)[:, None]
    u = mx_kscale(H)
    packed_xT = pack_weight(n((K, T)) * s)
    packed_eT = pack_weight(n((K, W)) * s)
    return {
        "x_words": packed_xT[0],
        "x_scales": packed_xT[1],
        "e_words": packed_eT[0],
        "e_scales": packed_eT[1],
        "w1": (n((K, H)) / np.sqrt(K) / s * u).astype(np.float32),
        "w2": (n((K, H)) / np.sqrt(K) / s).astype(np.float32),
        "w3": (n((H, N)) / np.sqrt(H) / u[:, None]).astype(np.float32),
        "bias": (0.5 * n((H, 1)) + 0.3).astype(np.float32),
        "offs": striped(np.random.permutation(T)[:S]),
        "tau": striped(np.random.permutation(W)[:U]),
        "whose": striped(np.random.randint(0, S, U)),
    }


def reference(x_words, x_scales, e_words, e_scales, w1, w2, w3, bias, offs, tau, whose):
    xq = unpack_weight(x_words, x_scales)[:, unstriped(offs)]
    h = relu(mxq(f64(w1), 0, "e4m3").T @ xq)
    e_tau = unpack_weight(e_words, e_scales)[:, unstriped(tau)]
    phi = relu((mxq(f64(w2), 0, "e4m3").T @ e_tau) + f64(bias))
    z = h[:, unstriped(whose)] * phi
    qv = mxq(f64(w3), 0, "e4m3").T @ mxq(z, 0, "e4m3")
    mq = qv.reshape(len(qv), -1, D).mean(axis=2)
    dv = np.abs(qv - np.repeat(mq, D, axis=1))
    return dv.reshape(len(dv), -1, D).mean(axis=2)

@@ -1,0 +1,186 @@
+from contextlib import ExitStack
+
+import concourse.mybir as mybir
+
+K, T, S, H, N, D = 512, 1024, 512, 512, 128, 4
+FLOPS = 2 * K * H * S * 2 + 2 * H * N * S
+
+F32 = mybir.dt.float32
+BF16 = mybir.dt.bfloat16
+I32 = mybir.dt.int32
+U32 = mybir.dt.uint32
+U16 = mybir.dt.uint16
+U8 = mybir.dt.uint8
+FP8X4 = mybir.dt.float8_e4m3fn_x4
+ACT = mybir.ActivationFunctionType
+ALU = mybir.AluOpType
+AXIS = mybir.AxisListType
+
+P = 128
+PACK = 4
+HALVES = 2
+R = S // HALVES
+E_ROW = 4
+
+
+def tile_picked_yiqn_dev_p_kernel(
+    tc, x_words, x_scales, e_words, e_scales, w1, w2, w3, bias, offs, tau, whose, out
+):
+    nc = tc.nc
+    with ExitStack() as ctx:
+        keep = ctx.enter_context(tc.tile_pool(name="keep", bufs=1))
+        psum = ctx.enter_context(tc.psum_pool(name="psum", bufs=1))
+
+        def sb(shape, dtype, name):
+            return keep.tile(shape, dtype, name=name, align_bytes=64)
+
+        offs_sb = keep.tile([P, S // 16], U16, name="offs_sb")
+        tau_sb = keep.tile([P, S // 16], U16, name="tau_sb")
+        whose_sb = keep.tile([P, S // 16], U16, name="whose_sb")
+
+        xs_all = sb([P, T], U8, "xs_all")
+        es_all = sb([P, T], U8, "es_all")
+        xw_all = sb([P, T], I32, "xw_all")
+        ew_all = sb([P, T], I32, "ew_all")
+        warm_in = sb([P, 1], F32, "warm_in")
+        warm_out = sb([P, 1], F32, "warm_out")
+        nc.vector.memset(xs_all[:].bitcast(I32), 0)
+        nc.vector.memset(es_all[:].bitcast(I32), 0)
+        nc.vector.memset(warm_in[:], 0.0)
+
+        def load_scales(queue, dst, src, row):
+            for q in range(4):
+                queue.dma_start(
+                    out=dst[32 * q + row : 32 * q + row + 4, :].bitcast(I32),
+                    in_=src[0, 4 * q : 4 * q + 4, :].bitcast(I32),
+                )
+
+        def load_words(dst, src):
+            nc.sync.dma_start(out=dst[:], in_=src[0].rearrange("p n t -> p (n t)").bitcast(I32))
+
+        def load_weight_half(w, c, name):
+            raw = sb([P, PACK, H // 2], F32, name)
+            nc.sync.dma_start(out=raw[:], in_=w.rearrange("(p j) n -> p j n", j=PACK)[:, :, c * (H // 2) : (c + 1) * (H // 2)])
+            return raw
+
+        nc.sync.dma_start(offs_sb[:], offs)
+        load_scales(nc.sync, xs_all, x_scales, 0)
+        load_words(xw_all, x_words)
+        w1_raw = [load_weight_half(w1, c, "w1_raw%d" % c) for c in range(2)]
+        load_scales(nc.gpsimd, es_all, e_scales, E_ROW)
+        nc.scalar.activation(warm_out[:], warm_in[:], ACT.Relu)
+        load_words(ew_all, e_words)
+        nc.sync.dma_start(tau_sb[:], tau)
+        w2_raw = [load_weight_half(w2, c, "w2_raw%d" % c) for c in range(2)]
+        nc.sync.dma_start(whose_sb[:], whose)
+        bias_sb = [sb([P, 1], F32, "bias_sb%d" % t) for t in range(PACK)]
+        bias_view = bias.rearrange("(g t i) o -> t g i o", t=PACK, i=4)
+        with nc.allow_non_contiguous_dma(reason="one float for each partition"):
+            for t in range(PACK):
+                nc.sync.dma_start(out=bias_sb[t][:], in_=bias_view[t])
+        w3_raw = sb([P, PACK, N], F32, "w3_raw")
+        w3_view = w3.rearrange("(g t i) n -> t g i n", t=PACK, i=4)
+        for t in range(PACK):
+            nc.sync.dma_start(out=w3_raw[:, t, :], in_=w3_view[t])
+
+        def gather_packed(words_all, scales_all, lst, name):
+            words = sb([P, S], U32, name + "_words")
+            scales = sb([P, S], U8, name + "_scales")
+            nc.vector.tensor_copy(scales[:], scales_all[:].indirect(lst[:]))
+            nc.vector.tensor_copy(words[:], words_all[:].bitcast(U32).indirect(lst[:]))
+            return words, scales
+
+        def round_weight_half(raw, c, grouped):
+            src = raw[:].rearrange("p j (g t i) -> p t g j i", t=PACK, i=4)
+            for t in range(PACK):
+                dst = grouped[t][:, c * (P // 2) : (c + 1) * (P // 2), :].rearrange("p (g i) j -> p g j i", i=4)
+                nc.scalar.copy(dst, src[:, t])
+
+        def quantize(grouped, width, name):
+            codes = sb([P, width], U32, name + "_codes")
+            scales = sb([P, width], U8, name + "_scales")
+            nc.vector.quantize_mx(out=codes[:].bitcast(FP8X4), scales=scales[:], in_=grouped[:].rearrange("p c j -> p (c j)"))
+            return codes, scales
+
+        def product(acc, lhs, rhs_codes, rhs_scales):
+            nc.tensor.matmul_mx(
+                out=acc, lhsT=lhs[0][:].bitcast(FP8X4), lhsT_scale=lhs[1][:],
+                rhs=rhs_codes.bitcast(FP8X4), rhs_scale=rhs_scales, start=True, stop=True,
+            )
+
+        xq = gather_packed(xw_all, xs_all, offs_sb, "xq")
+        w1_grouped = [sb([P, P, PACK], BF16, "w1_grouped%d" % t) for t in range(PACK)]
+        picked = [sb([P, PACK, R], F32, "picked%d" % a) for a in range(HALVES)]
+        w2_grouped = [sb([P, P, PACK], BF16, "w2_grouped%d" % t) for t in range(2)]
+        w2_grouped = w2_grouped + [picked[1][:, t, :].bitcast(BF16).rearrange("p (c j) -> p c j", j=PACK) for t in range(2, PACK)]
+        for c in range(2):
+            round_weight_half(w1_raw[c], c, w1_grouped)
+        h_acc = []
+        for t in range(PACK):
+            w1q = quantize(w1_grouped[t], P, "w1q%d" % t)
+            acc = psum.tile([P, S], F32, name="h_acc%d" % t, tag="bank%d" % t)
+            product(acc[:], w1q, xq[0][:], xq[1][:])
+            h_acc.append(acc)
+        eq = gather_packed(ew_all, es_all, tau_sb, "eq")
+
+        h = [sb([P, S], F32, "h%d" % t) for t in range(PACK)]
+
+        def pick(a, t):
+            nc.vector.tensor_copy(picked[a][:, t, :], h[t][:].indirect(whose_sb[:, a * (R // 16) : (a + 1) * (R // 16)]))
+
+        for t in range(PACK):
+            nc.scalar.activation(h[t][:], h_acc[t][:], ACT.Relu)
+            pick(0, t)
+
+        for c in range(2):
+            round_weight_half(w2_raw[c], c, w2_grouped)
+        phi_acc = []
+        for t in range(PACK):
+            w2q = quantize(w2_grouped[t], P, "w2q%d" % t)
+            acc = psum.tile([P, S], F32, name="phi_acc%d" % t, tag="bank%d" % (PACK + t))
+            product(acc[:], w2q, eq[0][:], eq[1][E_ROW:P, :])
+            phi_acc.append(acc)
+        for t in range(PACK):
+            pick(1, t)
+
+        w3_grouped = sb([P, N, PACK], BF16, "w3_grouped")
+        nc.scalar.activation(
+            w3_grouped[:].rearrange("p (c i) t -> p c t i", i=4),
+            w3_raw[:].rearrange("p t (c i) -> p c t i", i=4),
+            ACT.Copy, scale=1.0 / D,
+        )
+        w3q = quantize(w3_grouped, N, "w3q")
+
+        phi = [sb([P, PACK, R], F32, "phi%d" % a) for a in range(HALVES)]
+        for a in range(HALVES):
+            for t in range(PACK):
+                nc.scalar.activation(phi[a][:, t, :], phi_acc[t][:, a * R : (a + 1) * R], ACT.Relu, bias=bias_sb[t][:])
+
+        z = [sb([P, R, PACK], BF16, "z%d" % a) for a in range(HALVES)]
+        for a in range(HALVES):
+            nc.vector.tensor_tensor(
+                z[a][:].rearrange("p (c i) t -> p c t i", i=4),
+                picked[a][:].rearrange("p t (c i) -> p c t i", i=4),
+                phi[a][:].rearrange("p t (c i) -> p c t i", i=4),
+                ALU.mult,
+            )
+        qv = []
+        for a in range(HALVES):
+            zq = quantize(z[a], R, "zq%d" % a)
+            acc = psum.tile([P, R], F32, name="qv%d" % a, tag="bank%d" % a)
+            product(acc[:], w3q, zq[0][:], zq[1][:])
+            qv.append(acc[:].rearrange("p (v d) -> p v d", d=D))
+
+        V = R // D
+        mean = [sb([P, V], F32, "mean%d" % a) for a in range(HALVES)]
+        dev = [sb([P, V, D], F32, "dev%d" % a) for a in range(HALVES)]
+        result = sb([P, HALVES * V], F32, "result")
+        for a in range(HALVES):
+            nc.vector.tensor_reduce(mean[a][:], qv[a], AXIS.X, ALU.add)
+        for a in range(HALVES):
+            nc.vector.scalar_tensor_tensor(
+                dev[a][:], mean[a][:].unsqueeze(2).to_broadcast([P, V, D]), -1.0 / D, qv[a], ALU.mult, ALU.add
+            )
+        for a in range(HALVES):
+            nc.vector.tensor_reduce(result[:, a * V : (a + 1) * V], dev[a][:], AXIS.X, ALU.add, apply_absolute_value=True)
+        nc.sync.dma_start(out=out, in_=result[:])

@@ -20,7 +20,6 @@ P = 128
 PACK = 4
 HALVES = 2
 R = S // HALVES
-E_ROW = 4
 
 
 def tile_picked_yiqn_dev_p_kernel(
@@ -44,15 +43,14 @@ def tile_picked_yiqn_dev_p_kernel(
         ew_all = sb([P, T], I32, "ew_all")
         warm_in = sb([P, 1], F32, "warm_in")
         warm_out = sb([P, 1], F32, "warm_out")
-        nc.vector.memset(xs_all[:].bitcast(I32), 0)
-        nc.vector.memset(es_all[:].bitcast(I32), 0)
         nc.vector.memset(warm_in[:], 0.0)
 
-        def load_scales(queue, dst, src, row):
+        def load_scales(dst, src):
             for q in range(4):
-                queue.dma_start(
-                    out=dst[32 * q + row : 32 * q + row + 4, :].bitcast(I32),
-                    in_=src[0, 4 * q : 4 * q + 4, :].bitcast(I32),
+                rows = src[0, 4 * q : 4 * q + 4, :].bitcast(I32)
+                nc.sync.dma_start(
+                    out=dst[32 * q : 32 * q + 32, :].bitcast(I32),
+                    in_=rows.unsqueeze(0).to_broadcast([8, 4, T // 4]),
                 )
 
         def load_words(dst, src):
@@ -63,25 +61,27 @@ def tile_picked_yiqn_dev_p_kernel(
             nc.sync.dma_start(out=raw[:], in_=w.rearrange("(p j) n -> p j n", j=PACK)[:, :, c * (H // 2) : (c + 1) * (H // 2)])
             return raw
 
-        nc.sync.dma_start(offs_sb[:], offs)
-        load_scales(nc.sync, xs_all, x_scales, 0)
-        load_words(xw_all, x_words)
-        w1_raw = [load_weight_half(w1, c, "w1_raw%d" % c) for c in range(2)]
-        load_scales(nc.gpsimd, es_all, e_scales, E_ROW)
         nc.scalar.activation(warm_out[:], warm_in[:], ACT.Relu)
-        load_words(ew_all, e_words)
+        nc.sync.dma_start(offs_sb[:], offs)
+        load_scales(xs_all, x_scales)
+        load_words(xw_all, x_words)
+        w1_raw = [load_weight_half(w1, 0, "w1_raw0")]
         nc.sync.dma_start(tau_sb[:], tau)
-        w2_raw = [load_weight_half(w2, c, "w2_raw%d" % c) for c in range(2)]
+        load_scales(es_all, e_scales)
+        w1_raw.append(load_weight_half(w1, 1, "w1_raw1"))
+        load_words(ew_all, e_words)
+        w2_raw = [load_weight_half(w2, 0, "w2_raw0")]
         nc.sync.dma_start(whose_sb[:], whose)
+        w2_raw.append(load_weight_half(w2, 1, "w2_raw1"))
+        w3_raw = sb([P, PACK, N], F32, "w3_raw")
+        w3_view = w3.rearrange("(g t i) n -> t g i n", t=PACK, i=4)
+        for t in range(PACK):
+            nc.sync.dma_start(out=w3_raw[:, t, :], in_=w3_view[t])
         bias_sb = [sb([P, 1], F32, "bias_sb%d" % t) for t in range(PACK)]
         bias_view = bias.rearrange("(g t i) o -> t g i o", t=PACK, i=4)
         with nc.allow_non_contiguous_dma(reason="one float for each partition"):
             for t in range(PACK):
                 nc.sync.dma_start(out=bias_sb[t][:], in_=bias_view[t])
-        w3_raw = sb([P, PACK, N], F32, "w3_raw")
-        w3_view = w3.rearrange("(g t i) n -> t g i n", t=PACK, i=4)
-        for t in range(PACK):
-            nc.sync.dma_start(out=w3_raw[:, t, :], in_=w3_view[t])
 
         def gather_packed(words_all, scales_all, lst, name):
             words = sb([P, S], U32, name + "_words")
@@ -110,9 +110,9 @@ def tile_picked_yiqn_dev_p_kernel(
 
         xq = gather_packed(xw_all, xs_all, offs_sb, "xq")
         w1_grouped = [sb([P, P, PACK], BF16, "w1_grouped%d" % t) for t in range(PACK)]
-        picked = [sb([P, PACK, R], F32, "picked%d" % a) for a in range(HALVES)]
-        w2_grouped = [sb([P, P, PACK], BF16, "w2_grouped%d" % t) for t in range(2)]
-        w2_grouped = w2_grouped + [picked[1][:, t, :].bitcast(BF16).rearrange("p (c j) -> p c j", j=PACK) for t in range(2, PACK)]
+        picked = [sb([P, PACK * R], F32, "picked%d" % a) for a in range(HALVES)]
+        w2_all = picked[1][:].bitcast(BF16).rearrange("p (t c j) -> p t c j", t=PACK, j=PACK)
+        w2_grouped = [w2_all[:, t] for t in range(PACK)]
         for c in range(2):
             round_weight_half(w1_raw[c], c, w1_grouped)
         h_acc = []
@@ -121,47 +121,45 @@ def tile_picked_yiqn_dev_p_kernel(
             acc = psum.tile([P, S], F32, name="h_acc%d" % t, tag="bank%d" % t)
             product(acc[:], w1q, xq[0][:], xq[1][:])
             h_acc.append(acc)
+        nc.vector.tensor_copy(
+            w2_all[:, :, 0 : P // 2, :].rearrange("p t (g i) j -> p g t j i", i=4),
+            w2_raw[0][:].rearrange("p j (g t i) -> p g t j i", t=PACK, i=4),
+        )
         eq = gather_packed(ew_all, es_all, tau_sb, "eq")
 
         h = [sb([P, S], F32, "h%d" % t) for t in range(PACK)]
 
         def pick(a, t):
-            nc.vector.tensor_copy(picked[a][:, t, :], h[t][:].indirect(whose_sb[:, a * (R // 16) : (a + 1) * (R // 16)]))
+            nc.vector.tensor_copy(picked[a][:, t * R : (t + 1) * R], h[t][:].indirect(whose_sb[:, a * (R // 16) : (a + 1) * (R // 16)]))
 
         for t in range(PACK):
             nc.scalar.activation(h[t][:], h_acc[t][:], ACT.Relu)
             pick(0, t)
 
-        for c in range(2):
-            round_weight_half(w2_raw[c], c, w2_grouped)
-        phi_acc = []
+        round_weight_half(w2_raw[1], 1, w2_grouped)
+        phi = sb([P, PACK, S], F32, "phi")
         for t in range(PACK):
             w2q = quantize(w2_grouped[t], P, "w2q%d" % t)
             acc = psum.tile([P, S], F32, name="phi_acc%d" % t, tag="bank%d" % (PACK + t))
-            product(acc[:], w2q, eq[0][:], eq[1][E_ROW:P, :])
-            phi_acc.append(acc)
+            product(acc[:], w2q, eq[0][:], eq[1][:])
+            nc.scalar.activation(phi[:, t, :], acc[:], ACT.Relu, bias=bias_sb[t][:])
         for t in range(PACK):
             pick(1, t)
 
         w3_grouped = sb([P, N, PACK], BF16, "w3_grouped")
-        nc.scalar.activation(
+        nc.vector.tensor_scalar_mul(
             w3_grouped[:].rearrange("p (c i) t -> p c t i", i=4),
             w3_raw[:].rearrange("p t (c i) -> p c t i", i=4),
-            ACT.Copy, scale=1.0 / D,
+            1.0 / D,
         )
         w3q = quantize(w3_grouped, N, "w3q")
-
-        phi = [sb([P, PACK, R], F32, "phi%d" % a) for a in range(HALVES)]
-        for a in range(HALVES):
-            for t in range(PACK):
-                nc.scalar.activation(phi[a][:, t, :], phi_acc[t][:, a * R : (a + 1) * R], ACT.Relu, bias=bias_sb[t][:])
 
         z = [sb([P, R, PACK], BF16, "z%d" % a) for a in range(HALVES)]
         for a in range(HALVES):
             nc.vector.tensor_tensor(
                 z[a][:].rearrange("p (c i) t -> p c t i", i=4),
-                picked[a][:].rearrange("p t (c i) -> p c t i", i=4),
-                phi[a][:].rearrange("p t (c i) -> p c t i", i=4),
+                picked[a][:].rearrange("p (t c i) -> p c t i", t=PACK, i=4),
+                phi[:, :, a * R : (a + 1) * R].rearrange("p t (c i) -> p c t i", i=4),
                 ALU.mult,
             )
         qv = []

@@ -20,6 +20,7 @@ P = 128
 PACK = 4
 HALVES = 2
 R = S // HALVES
+PARTS = ((0, 256), (256, 128), (384, 128))
 
 
 def tile_picked_yiqn_dev_p_kernel(
@@ -45,10 +46,10 @@ def tile_picked_yiqn_dev_p_kernel(
         warm_out = sb([P, 1], F32, "warm_out")
         nc.vector.memset(warm_in[:], 0.0)
 
-        def load_scales(dst, src):
+        def load_scales(queue, dst, src):
             for q in range(4):
                 rows = src[0, 4 * q : 4 * q + 4, :].bitcast(I32)
-                nc.sync.dma_start(
+                queue.dma_start(
                     out=dst[32 * q : 32 * q + 32, :].bitcast(I32),
                     in_=rows.unsqueeze(0).to_broadcast([8, 4, T // 4]),
                 )
@@ -63,11 +64,11 @@ def tile_picked_yiqn_dev_p_kernel(
 
         nc.scalar.activation(warm_out[:], warm_in[:], ACT.Relu)
         nc.sync.dma_start(offs_sb[:], offs)
-        load_scales(xs_all, x_scales)
+        load_scales(nc.sync, xs_all, x_scales)
         load_words(xw_all, x_words)
         w1_raw = [load_weight_half(w1, 0, "w1_raw0")]
         nc.sync.dma_start(tau_sb[:], tau)
-        load_scales(es_all, e_scales)
+        load_scales(nc.sync, es_all, e_scales)
         w1_raw.append(load_weight_half(w1, 1, "w1_raw1"))
         load_words(ew_all, e_words)
         w2_raw = [load_weight_half(w2, 0, "w2_raw0")]
@@ -81,7 +82,7 @@ def tile_picked_yiqn_dev_p_kernel(
         bias_view = bias.rearrange("(g t i) o -> t g i o", t=PACK, i=4)
         with nc.allow_non_contiguous_dma(reason="one float for each partition"):
             for t in range(PACK):
-                nc.sync.dma_start(out=bias_sb[t][:], in_=bias_view[t])
+                nc.gpsimd.dma_start(out=bias_sb[t][:], in_=bias_view[t])
 
         def gather_packed(words_all, scales_all, lst, name):
             words = sb([P, S], U32, name + "_words")
@@ -111,8 +112,9 @@ def tile_picked_yiqn_dev_p_kernel(
         xq = gather_packed(xw_all, xs_all, offs_sb, "xq")
         w1_grouped = [sb([P, P, PACK], BF16, "w1_grouped%d" % t) for t in range(PACK)]
         picked = [sb([P, PACK * R], F32, "picked%d" % a) for a in range(HALVES)]
-        w2_all = picked[1][:].bitcast(BF16).rearrange("p (t c j) -> p t c j", t=PACK, j=PACK)
-        w2_grouped = [w2_all[:, t] for t in range(PACK)]
+        w2_grouped = [sb([P, P, PACK], BF16, "w2_grouped%d" % t) for t in range(PACK - 1)]
+        shared = picked[1][:, 5 * R // 2 : 7 * R // 2]
+        w2_grouped.append(shared.bitcast(BF16).rearrange("p (c j) -> p c j", j=PACK))
         for c in range(2):
             round_weight_half(w1_raw[c], c, w1_grouped)
         h_acc = []
@@ -121,10 +123,6 @@ def tile_picked_yiqn_dev_p_kernel(
             acc = psum.tile([P, S], F32, name="h_acc%d" % t, tag="bank%d" % t)
             product(acc[:], w1q, xq[0][:], xq[1][:])
             h_acc.append(acc)
-        nc.vector.tensor_copy(
-            w2_all[:, :, 0 : P // 2, :].rearrange("p t (g i) j -> p g t j i", i=4),
-            w2_raw[0][:].rearrange("p j (g t i) -> p g t j i", t=PACK, i=4),
-        )
         eq = gather_packed(ew_all, es_all, tau_sb, "eq")
 
         h = [sb([P, S], F32, "h%d" % t) for t in range(PACK)]
@@ -136,49 +134,56 @@ def tile_picked_yiqn_dev_p_kernel(
             nc.scalar.activation(h[t][:], h_acc[t][:], ACT.Relu)
             pick(0, t)
 
-        round_weight_half(w2_raw[1], 1, w2_grouped)
-        phi = sb([P, PACK, S], F32, "phi")
+        for c in range(2):
+            round_weight_half(w2_raw[c], c, w2_grouped)
+        phi_acc = []
         for t in range(PACK):
             w2q = quantize(w2_grouped[t], P, "w2q%d" % t)
             acc = psum.tile([P, S], F32, name="phi_acc%d" % t, tag="bank%d" % (PACK + t))
             product(acc[:], w2q, eq[0][:], eq[1][:])
-            nc.scalar.activation(phi[:, t, :], acc[:], ACT.Relu, bias=bias_sb[t][:])
+            phi_acc.append(acc)
         for t in range(PACK):
             pick(1, t)
 
         w3_grouped = sb([P, N, PACK], BF16, "w3_grouped")
-        nc.vector.tensor_scalar_mul(
+        nc.scalar.activation(
             w3_grouped[:].rearrange("p (c i) t -> p c t i", i=4),
             w3_raw[:].rearrange("p t (c i) -> p c t i", i=4),
-            1.0 / D,
+            ACT.Copy, scale=1.0 / D,
         )
         w3q = quantize(w3_grouped, N, "w3q")
 
-        z = [sb([P, R, PACK], BF16, "z%d" % a) for a in range(HALVES)]
-        for a in range(HALVES):
-            nc.vector.tensor_tensor(
-                z[a][:].rearrange("p (c i) t -> p c t i", i=4),
-                picked[a][:].rearrange("p (t c i) -> p c t i", t=PACK, i=4),
-                phi[:, :, a * R : (a + 1) * R].rearrange("p t (c i) -> p c t i", i=4),
-                ALU.mult,
+        z = []
+        for n, (first, width) in enumerate(PARTS):
+            signed = sb([P, PACK, width], F32, "signed%d" % n)
+            a, c0 = divmod(first, R)
+            for t in range(PACK):
+                nc.vector.scalar_tensor_tensor(
+                    signed[:, t, :], phi_acc[t][:, first : first + width], bias_sb[t][:],
+                    picked[a][:, t * R + c0 : t * R + c0 + width], ALU.add, ALU.mult,
+                )
+            grouped = sb([P, width, PACK], BF16, "z%d" % n)
+            nc.scalar.activation(
+                grouped[:].rearrange("p (c i) t -> p c t i", i=4),
+                signed[:].rearrange("p t (c i) -> p c t i", i=4),
+                ACT.Relu,
             )
+            z.append(grouped)
         qv = []
-        for a in range(HALVES):
-            zq = quantize(z[a], R, "zq%d" % a)
-            acc = psum.tile([P, R], F32, name="qv%d" % a, tag="bank%d" % a)
+        for n, (first, width) in enumerate(PARTS):
+            zq = quantize(z[n], width, "zq%d" % n)
+            acc = psum.tile([P, width], F32, name="qv%d" % n, tag="bank%d" % n)
             product(acc[:], w3q, zq[0][:], zq[1][:])
             qv.append(acc[:].rearrange("p (v d) -> p v d", d=D))
 
-        V = R // D
-        mean = [sb([P, V], F32, "mean%d" % a) for a in range(HALVES)]
-        dev = [sb([P, V, D], F32, "dev%d" % a) for a in range(HALVES)]
-        result = sb([P, HALVES * V], F32, "result")
-        for a in range(HALVES):
-            nc.vector.tensor_reduce(mean[a][:], qv[a], AXIS.X, ALU.add)
-        for a in range(HALVES):
+        result = sb([P, S // D], F32, "result")
+        for n, (first, width) in enumerate(PARTS):
+            v = width // D
+            mean = sb([P, v], F32, "mean%d" % n)
+            dev = sb([P, v, D], F32, "dev%d" % n)
+            nc.vector.tensor_reduce(mean[:], qv[n], AXIS.X, ALU.add)
             nc.vector.scalar_tensor_tensor(
-                dev[a][:], mean[a][:].unsqueeze(2).to_broadcast([P, V, D]), -1.0 / D, qv[a], ALU.mult, ALU.add
+                dev[:], mean[:].unsqueeze(2).to_broadcast([P, v, D]), -1.0 / D, qv[n], ALU.mult, ALU.add
             )
-        for a in range(HALVES):
-            nc.vector.tensor_reduce(result[:, a * V : (a + 1) * V], dev[a][:], AXIS.X, ALU.add, apply_absolute_value=True)
+            nc.vector.tensor_reduce(result[:, first // D : first // D + v], dev[:], AXIS.X, ALU.add, apply_absolute_value=True)
         nc.sync.dma_start(out=out, in_=result[:])

@@ -3,7 +3,7 @@ from contextlib import ExitStack
 import concourse.mybir as mybir
 
 K, T, S, H, N, D = 512, 1024, 512, 512, 128, 4
-FLOPS = 2 * K * H * S * 2 + 2 * H * N * S
+FLOPS = 2 * (2 * K * H * S) + 2 * H * N * S
 
 F32 = mybir.dt.float32
 BF16 = mybir.dt.bfloat16
@@ -18,9 +18,12 @@ AXIS = mybir.AxisListType
 
 P = 128
 PACK = 4
+RUN = 4
+QUADRANT = 32
+PER_COLUMN = 16
 HALVES = 2
 R = S // HALVES
-PARTS = ((0, 256), (256, 128), (384, 128))
+V = R // D
 
 
 def tile_picked_yiqn_dev_p_kernel(
@@ -31,159 +34,167 @@ def tile_picked_yiqn_dev_p_kernel(
         keep = ctx.enter_context(tc.tile_pool(name="keep", bufs=1))
         psum = ctx.enter_context(tc.psum_pool(name="psum", bufs=1))
 
-        def sb(shape, dtype, name):
-            return keep.tile(shape, dtype, name=name, align_bytes=64)
+        def sb(shape, dtype, name, tag=None):
+            return keep.tile(shape, dtype, name=name, tag=tag or name, align_bytes=64)
 
-        offs_sb = keep.tile([P, S // 16], U16, name="offs_sb")
-        tau_sb = keep.tile([P, S // 16], U16, name="tau_sb")
-        whose_sb = keep.tile([P, S // 16], U16, name="whose_sb")
-
+        offs_sb = keep.tile([P, S // PER_COLUMN], U16, name="offs_sb")
+        tau_sb = keep.tile([P, S // PER_COLUMN], U16, name="tau_sb")
+        whose_sb = keep.tile([P, S // PER_COLUMN], U16, name="whose_sb")
         xs_all = sb([P, T], U8, "xs_all")
         es_all = sb([P, T], U8, "es_all")
         xw_all = sb([P, T], I32, "xw_all")
         ew_all = sb([P, T], I32, "ew_all")
+
         warm_in = sb([P, 1], F32, "warm_in")
         warm_out = sb([P, 1], F32, "warm_out")
         nc.vector.memset(warm_in[:], 0.0)
+        nc.scalar.activation(warm_out[:], warm_in[:], ACT.Relu)
 
-        def load_scales(queue, dst, src):
-            for q in range(4):
+        def load_scales(dst, src):
+            for q in range(P // QUADRANT):
                 rows = src[0, 4 * q : 4 * q + 4, :].bitcast(I32)
-                queue.dma_start(
-                    out=dst[32 * q : 32 * q + 32, :].bitcast(I32),
-                    in_=rows.unsqueeze(0).to_broadcast([8, 4, T // 4]),
+                nc.sync.dma_start(
+                    out=dst[QUADRANT * q : QUADRANT * (q + 1), :].bitcast(I32),
+                    in_=rows.unsqueeze(0).to_broadcast([QUADRANT // 4, 4, T // 4]),
                 )
 
         def load_words(dst, src):
             nc.sync.dma_start(out=dst[:], in_=src[0].rearrange("p n t -> p (n t)").bitcast(I32))
 
-        def load_weight_half(w, c, name):
-            raw = sb([P, PACK, H // 2], F32, name)
-            nc.sync.dma_start(out=raw[:], in_=w.rearrange("(p j) n -> p j n", j=PACK)[:, :, c * (H // 2) : (c + 1) * (H // 2)])
+        def load_w1_half(c):
+            raw = sb([P, PACK, H // 2], F32, "w1_raw%d" % c)
+            cols = slice(c * (H // 2), (c + 1) * (H // 2))
+            nc.sync.dma_start(out=raw[:], in_=w1.rearrange("(p j) n -> p j n", j=PACK)[:, :, cols])
             return raw
 
-        nc.scalar.activation(warm_out[:], warm_in[:], ACT.Relu)
         nc.sync.dma_start(offs_sb[:], offs)
-        load_scales(nc.sync, xs_all, x_scales)
+        load_scales(xs_all, x_scales)
         load_words(xw_all, x_words)
-        w1_raw = [load_weight_half(w1, 0, "w1_raw0")]
+        w1_raw = [load_w1_half(0)]
         nc.sync.dma_start(tau_sb[:], tau)
-        load_scales(nc.sync, es_all, e_scales)
-        w1_raw.append(load_weight_half(w1, 1, "w1_raw1"))
+        load_scales(es_all, e_scales)
+        w1_raw.append(load_w1_half(1))
         load_words(ew_all, e_words)
-        w2_raw = [load_weight_half(w2, 0, "w2_raw0")]
+        w2_raw = sb([P, PACK, H], F32, "w2_raw")
+        nc.sync.dma_start(out=w2_raw[:], in_=w2.rearrange("(p j) n -> p j n", j=PACK))
         nc.sync.dma_start(whose_sb[:], whose)
-        w2_raw.append(load_weight_half(w2, 1, "w2_raw1"))
         w3_raw = sb([P, PACK, N], F32, "w3_raw")
-        w3_view = w3.rearrange("(g t i) n -> t g i n", t=PACK, i=4)
+        w3_view = w3.rearrange("(g t e) n -> t g e n", t=PACK, e=RUN)
         for t in range(PACK):
             nc.sync.dma_start(out=w3_raw[:, t, :], in_=w3_view[t])
         bias_sb = [sb([P, 1], F32, "bias_sb%d" % t) for t in range(PACK)]
-        bias_view = bias.rearrange("(g t i) o -> t g i o", t=PACK, i=4)
+        bias_view = bias.rearrange("(g t e) o -> t g e o", t=PACK, e=RUN)
         with nc.allow_non_contiguous_dma(reason="one float for each partition"):
             for t in range(PACK):
-                nc.gpsimd.dma_start(out=bias_sb[t][:], in_=bias_view[t])
+                nc.sync.dma_start(out=bias_sb[t][:], in_=bias_view[t])
 
-        def gather_packed(words_all, scales_all, lst, name):
+        def gather_packed(words_all, scales_all, entries, name):
             words = sb([P, S], U32, name + "_words")
             scales = sb([P, S], U8, name + "_scales")
-            nc.vector.tensor_copy(scales[:], scales_all[:].indirect(lst[:]))
-            nc.vector.tensor_copy(words[:], words_all[:].bitcast(U32).indirect(lst[:]))
+            nc.vector.tensor_copy(scales[:], scales_all[:].indirect(entries[:]))
+            nc.vector.tensor_copy(words[:], words_all[:].bitcast(U32).indirect(entries[:]))
             return words, scales
 
-        def round_weight_half(raw, c, grouped):
-            src = raw[:].rearrange("p j (g t i) -> p t g j i", t=PACK, i=4)
-            for t in range(PACK):
-                dst = grouped[t][:, c * (P // 2) : (c + 1) * (P // 2), :].rearrange("p (g i) j -> p g j i", i=4)
-                nc.scalar.copy(dst, src[:, t])
+        def channel_tiles(raw):
+            return raw[:].rearrange("p j (g t e) -> p t g j e", t=PACK, e=RUN)
+
+        def as_written(grouped):
+            return grouped.rearrange("p (g e) j -> p g j e", e=RUN)
 
         def quantize(grouped, width, name):
             codes = sb([P, width], U32, name + "_codes")
             scales = sb([P, width], U8, name + "_scales")
-            nc.vector.quantize_mx(out=codes[:].bitcast(FP8X4), scales=scales[:], in_=grouped[:].rearrange("p c j -> p (c j)"))
+            nc.vector.quantize_mx(
+                out=codes[:].bitcast(FP8X4), scales=scales[:], in_=grouped[:].rearrange("p c j -> p (c j)")
+            )
             return codes, scales
 
-        def product(acc, lhs, rhs_codes, rhs_scales):
+        def product(acc, stationary, moving):
             nc.tensor.matmul_mx(
-                out=acc, lhsT=lhs[0][:].bitcast(FP8X4), lhsT_scale=lhs[1][:],
-                rhs=rhs_codes.bitcast(FP8X4), rhs_scale=rhs_scales, start=True, stop=True,
+                out=acc[:],
+                lhsT=stationary[0][:].bitcast(FP8X4),
+                lhsT_scale=stationary[1][:],
+                rhs=moving[0][:].bitcast(FP8X4),
+                rhs_scale=moving[1][:],
+                start=True,
+                stop=True,
             )
 
         xq = gather_packed(xw_all, xs_all, offs_sb, "xq")
         w1_grouped = [sb([P, P, PACK], BF16, "w1_grouped%d" % t) for t in range(PACK)]
-        picked = [sb([P, PACK * R], F32, "picked%d" % a) for a in range(HALVES)]
-        w2_grouped = [sb([P, P, PACK], BF16, "w2_grouped%d" % t) for t in range(PACK - 1)]
-        shared = picked[1][:, 5 * R // 2 : 7 * R // 2]
-        w2_grouped.append(shared.bitcast(BF16).rearrange("p (c j) -> p c j", j=PACK))
+
+        shared = sb([P, PACK * R + R // 2], F32, "shared")
+        picked = [sb([P, PACK * R], F32, "picked0")[:], shared[:, R // 2 :]]
+        w2_grouped = [
+            shared[:, t * R : (t + 1) * R].bitcast(BF16).rearrange("p (c j) -> p c j", j=PACK) for t in range(PACK)
+        ]
+
         for c in range(2):
-            round_weight_half(w1_raw[c], c, w1_grouped)
+            for t in range(PACK):
+                nc.scalar.copy(as_written(w1_grouped[t][:, c * (P // 2) : (c + 1) * (P // 2), :]), channel_tiles(w1_raw[c])[:, t])
         h_acc = []
         for t in range(PACK):
             w1q = quantize(w1_grouped[t], P, "w1q%d" % t)
             acc = psum.tile([P, S], F32, name="h_acc%d" % t, tag="bank%d" % t)
-            product(acc[:], w1q, xq[0][:], xq[1][:])
+            product(acc, w1q, xq)
             h_acc.append(acc)
         eq = gather_packed(ew_all, es_all, tau_sb, "eq")
 
         h = [sb([P, S], F32, "h%d" % t) for t in range(PACK)]
 
         def pick(a, t):
-            nc.vector.tensor_copy(picked[a][:, t * R : (t + 1) * R], h[t][:].indirect(whose_sb[:, a * (R // 16) : (a + 1) * (R // 16)]))
+            entries = whose_sb[:, a * (R // PER_COLUMN) : (a + 1) * (R // PER_COLUMN)]
+            nc.vector.tensor_copy(picked[a][:, t * R : (t + 1) * R], h[t][:].indirect(entries))
 
         for t in range(PACK):
             nc.scalar.activation(h[t][:], h_acc[t][:], ACT.Relu)
             pick(0, t)
 
-        for c in range(2):
-            round_weight_half(w2_raw[c], c, w2_grouped)
-        phi_acc = []
+        for t in range(PACK):
+            nc.scalar.copy(as_written(w2_grouped[t]), channel_tiles(w2_raw)[:, t])
+        phi = sb([P, PACK, S], F32, "phi")
         for t in range(PACK):
             w2q = quantize(w2_grouped[t], P, "w2q%d" % t)
             acc = psum.tile([P, S], F32, name="phi_acc%d" % t, tag="bank%d" % (PACK + t))
-            product(acc[:], w2q, eq[0][:], eq[1][:])
-            phi_acc.append(acc)
+            product(acc, w2q, eq)
+            nc.scalar.activation(phi[:, t, :], acc[:], ACT.Relu, bias=bias_sb[t][:])
         for t in range(PACK):
             pick(1, t)
 
-        w3_grouped = sb([P, N, PACK], BF16, "w3_grouped")
-        nc.scalar.activation(
-            w3_grouped[:].rearrange("p (c i) t -> p c t i", i=4),
-            w3_raw[:].rearrange("p t (c i) -> p c t i", i=4),
-            ACT.Copy, scale=1.0 / D,
+        w3_grouped = sb([P, N, PACK], BF16, "w3_grouped", tag="w2_raw")
+        nc.vector.tensor_scalar_mul(
+            w3_grouped[:].rearrange("p (c e) t -> p c t e", e=RUN),
+            w3_raw[:].rearrange("p t (c e) -> p c t e", e=RUN),
+            1.0 / D,
         )
         w3q = quantize(w3_grouped, N, "w3q")
 
-        z = []
-        for n, (first, width) in enumerate(PARTS):
-            signed = sb([P, PACK, width], F32, "signed%d" % n)
-            a, c0 = divmod(first, R)
-            for t in range(PACK):
-                nc.vector.scalar_tensor_tensor(
-                    signed[:, t, :], phi_acc[t][:, first : first + width], bias_sb[t][:],
-                    picked[a][:, t * R + c0 : t * R + c0 + width], ALU.add, ALU.mult,
-                )
-            grouped = sb([P, width, PACK], BF16, "z%d" % n)
-            nc.scalar.activation(
-                grouped[:].rearrange("p (c i) t -> p c t i", i=4),
-                signed[:].rearrange("p t (c i) -> p c t i", i=4),
-                ACT.Relu,
+        z = [sb([P, R, PACK], BF16, "z%d" % a) for a in range(HALVES)]
+        for a in range(HALVES):
+            nc.vector.tensor_tensor(
+                z[a][:].rearrange("p (c e) t -> p c t e", e=RUN),
+                picked[a].rearrange("p (t c e) -> p c t e", t=PACK, e=RUN),
+                phi[:, :, a * R : (a + 1) * R].rearrange("p t (c e) -> p c t e", e=RUN),
+                ALU.mult,
             )
-            z.append(grouped)
-        qv = []
-        for n, (first, width) in enumerate(PARTS):
-            zq = quantize(z[n], width, "zq%d" % n)
-            acc = psum.tile([P, width], F32, name="qv%d" % n, tag="bank%d" % n)
-            product(acc[:], w3q, zq[0][:], zq[1][:])
-            qv.append(acc[:].rearrange("p (v d) -> p v d", d=D))
+        qv_scaled = []
+        for a in range(HALVES):
+            zq = quantize(z[a], R, "zq%d" % a)
+            acc = psum.tile([P, R], F32, name="qv%d" % a, tag="bank%d" % a)
+            product(acc, w3q, zq)
+            qv_scaled.append(acc[:].rearrange("p (v d) -> p v d", d=D))
 
-        result = sb([P, S // D], F32, "result")
-        for n, (first, width) in enumerate(PARTS):
-            v = width // D
-            mean = sb([P, v], F32, "mean%d" % n)
-            dev = sb([P, v, D], F32, "dev%d" % n)
-            nc.vector.tensor_reduce(mean[:], qv[n], AXIS.X, ALU.add)
+        mq = [sb([P, V], F32, "mq%d" % a) for a in range(HALVES)]
+        dev = [sb([P, V, D], F32, "dev%d" % a) for a in range(HALVES)]
+        result = sb([P, HALVES * V], F32, "result")
+        for a in range(HALVES):
+            nc.vector.tensor_reduce(mq[a][:], qv_scaled[a], AXIS.X, ALU.add)
+        for a in range(HALVES):
             nc.vector.scalar_tensor_tensor(
-                dev[:], mean[:].unsqueeze(2).to_broadcast([P, v, D]), -1.0 / D, qv[n], ALU.mult, ALU.add
+                dev[a][:], mq[a][:].unsqueeze(2).to_broadcast([P, V, D]), -1.0 / D, qv_scaled[a], ALU.mult, ALU.add
             )
-            nc.vector.tensor_reduce(result[:, first // D : first // D + v], dev[:], AXIS.X, ALU.add, apply_absolute_value=True)
+        for a in range(HALVES):
+            nc.vector.tensor_reduce(
+                result[:, a * V : (a + 1) * V], dev[a][:], AXIS.X, ALU.add, apply_absolute_value=True
+            )
         nc.sync.dma_start(out=out, in_=result[:])

@@ -61,23 +61,23 @@ def tile_picked_yiqn_dev_p_kernel(
         def load_words(dst, src):
             nc.sync.dma_start(out=dst[:], in_=src[0].rearrange("p n t -> p (n t)").bitcast(I32))
 
-        def load_w1_half(c):
-            raw = sb([P, PACK, H // 2], F32, "w1_raw%d" % c)
+        def load_weight_half(w, c, name):
+            raw = sb([P, PACK, H // 2], F32, "%s_raw%d" % (name, c))
             cols = slice(c * (H // 2), (c + 1) * (H // 2))
-            nc.sync.dma_start(out=raw[:], in_=w1.rearrange("(p j) n -> p j n", j=PACK)[:, :, cols])
+            nc.sync.dma_start(out=raw[:], in_=w.rearrange("(p j) n -> p j n", j=PACK)[:, :, cols])
             return raw
 
         nc.sync.dma_start(offs_sb[:], offs)
         load_scales(xs_all, x_scales)
         load_words(xw_all, x_words)
-        w1_raw = [load_w1_half(0)]
+        w1_raw = [load_weight_half(w1, 0, "w1")]
         nc.sync.dma_start(tau_sb[:], tau)
         load_scales(es_all, e_scales)
-        w1_raw.append(load_w1_half(1))
+        w1_raw.append(load_weight_half(w1, 1, "w1"))
         load_words(ew_all, e_words)
-        w2_raw = sb([P, PACK, H], F32, "w2_raw")
-        nc.sync.dma_start(out=w2_raw[:], in_=w2.rearrange("(p j) n -> p j n", j=PACK))
+        w2_raw = [load_weight_half(w2, 0, "w2")]
         nc.sync.dma_start(whose_sb[:], whose)
+        w2_raw.append(load_weight_half(w2, 1, "w2"))
         w3_raw = sb([P, PACK, N], F32, "w3_raw")
         w3_view = w3.rearrange("(g t e) n -> t g e n", t=PACK, e=RUN)
         for t in range(PACK):
@@ -95,11 +95,11 @@ def tile_picked_yiqn_dev_p_kernel(
             nc.vector.tensor_copy(words[:], words_all[:].bitcast(U32).indirect(entries[:]))
             return words, scales
 
-        def channel_tiles(raw):
-            return raw[:].rearrange("p j (g t e) -> p t g j e", t=PACK, e=RUN)
-
-        def as_written(grouped):
-            return grouped.rearrange("p (g e) j -> p g j e", e=RUN)
+        def round_half_on_scalar(raw, c, grouped):
+            src = raw[:].rearrange("p j (g t e) -> p t g j e", t=PACK, e=RUN)
+            for t in range(PACK):
+                dst = grouped[t][:, c * (P // 2) : (c + 1) * (P // 2), :].rearrange("p (g e) j -> p g j e", e=RUN)
+                nc.scalar.copy(dst, src[:, t])
 
         def quantize(grouped, width, name):
             codes = sb([P, width], U32, name + "_codes")
@@ -123,21 +123,22 @@ def tile_picked_yiqn_dev_p_kernel(
         xq = gather_packed(xw_all, xs_all, offs_sb, "xq")
         w1_grouped = [sb([P, P, PACK], BF16, "w1_grouped%d" % t) for t in range(PACK)]
 
-        shared = sb([P, PACK * R + R // 2], F32, "shared")
-        picked = [sb([P, PACK * R], F32, "picked0")[:], shared[:, R // 2 :]]
-        w2_grouped = [
-            shared[:, t * R : (t + 1) * R].bitcast(BF16).rearrange("p (c j) -> p c j", j=PACK) for t in range(PACK)
-        ]
+        picked = [sb([P, PACK * R], F32, "picked%d" % a) for a in range(HALVES)]
+        w2_all = picked[1][:].bitcast(BF16).rearrange("p (t c j) -> p t c j", t=PACK, j=PACK)
+        w2_grouped = [w2_all[:, t] for t in range(PACK)]
 
         for c in range(2):
-            for t in range(PACK):
-                nc.scalar.copy(as_written(w1_grouped[t][:, c * (P // 2) : (c + 1) * (P // 2), :]), channel_tiles(w1_raw[c])[:, t])
+            round_half_on_scalar(w1_raw[c], c, w1_grouped)
         h_acc = []
         for t in range(PACK):
             w1q = quantize(w1_grouped[t], P, "w1q%d" % t)
             acc = psum.tile([P, S], F32, name="h_acc%d" % t, tag="bank%d" % t)
             product(acc, w1q, xq)
             h_acc.append(acc)
+        nc.vector.tensor_copy(
+            w2_all[:, :, 0 : P // 2, :].rearrange("p t (g e) j -> p g t j e", e=RUN),
+            w2_raw[0][:].rearrange("p j (g t e) -> p g t j e", t=PACK, e=RUN),
+        )
         eq = gather_packed(ew_all, es_all, tau_sb, "eq")
 
         h = [sb([P, S], F32, "h%d" % t) for t in range(PACK)]
@@ -150,22 +151,24 @@ def tile_picked_yiqn_dev_p_kernel(
             nc.scalar.activation(h[t][:], h_acc[t][:], ACT.Relu)
             pick(0, t)
 
-        for t in range(PACK):
-            nc.scalar.copy(as_written(w2_grouped[t]), channel_tiles(w2_raw)[:, t])
+        round_half_on_scalar(w2_raw[1], 1, w2_grouped)
         phi = sb([P, PACK, S], F32, "phi")
         for t in range(PACK):
             w2q = quantize(w2_grouped[t], P, "w2q%d" % t)
             acc = psum.tile([P, S], F32, name="phi_acc%d" % t, tag="bank%d" % (PACK + t))
             product(acc, w2q, eq)
-            nc.scalar.activation(phi[:, t, :], acc[:], ACT.Relu, bias=bias_sb[t][:])
+            step = R if t == PACK - 1 else S
+            for c0 in range(0, S, step):
+                nc.scalar.activation(phi[:, t, c0 : c0 + step], acc[:, c0 : c0 + step], ACT.Relu, bias=bias_sb[t][:])
         for t in range(PACK):
             pick(1, t)
 
-        w3_grouped = sb([P, N, PACK], BF16, "w3_grouped", tag="w2_raw")
-        nc.vector.tensor_scalar_mul(
+        w3_grouped = sb([P, N, PACK], BF16, "w3_grouped", tag="bias_sb%d" % (PACK - 1))
+        nc.scalar.activation(
             w3_grouped[:].rearrange("p (c e) t -> p c t e", e=RUN),
             w3_raw[:].rearrange("p t (c e) -> p c t e", e=RUN),
-            1.0 / D,
+            ACT.Copy,
+            scale=1.0 / D,
         )
         w3q = quantize(w3_grouped, N, "w3q")
 
@@ -173,7 +176,7 @@ def tile_picked_yiqn_dev_p_kernel(
         for a in range(HALVES):
             nc.vector.tensor_tensor(
                 z[a][:].rearrange("p (c e) t -> p c t e", e=RUN),
-                picked[a].rearrange("p (t c e) -> p c t e", t=PACK, e=RUN),
+                picked[a][:].rearrange("p (t c e) -> p c t e", t=PACK, e=RUN),
                 phi[:, :, a * R : (a + 1) * R].rearrange("p t (c e) -> p c t e", e=RUN),
                 ALU.mult,
             )

from contextlib import ExitStack

import concourse.mybir as mybir

K, T, S, H, N, D = 512, 1024, 512, 512, 128, 4
FLOPS = 2 * (2 * K * H * S) + 2 * H * N * S

F32 = mybir.dt.float32
BF16 = mybir.dt.bfloat16
I32 = mybir.dt.int32
U32 = mybir.dt.uint32
U16 = mybir.dt.uint16
U8 = mybir.dt.uint8
FP8X4 = mybir.dt.float8_e4m3fn_x4
ACT = mybir.ActivationFunctionType
ALU = mybir.AluOpType
AXIS = mybir.AxisListType

P = 128
PACK = 4
RUN = 4
QUADRANT = 32
PER_COLUMN = 16
HALVES = 2
R = S // HALVES
V = R // D


def tile_picked_yiqn_dev_p_kernel(
    tc, x_words, x_scales, e_words, e_scales, w1, w2, w3, bias, offs, tau, whose, out
):
    nc = tc.nc
    with ExitStack() as ctx:
        keep = ctx.enter_context(tc.tile_pool(name="keep", bufs=1))
        psum = ctx.enter_context(tc.psum_pool(name="psum", bufs=1))

        def sb(shape, dtype, name, tag=None):
            return keep.tile(shape, dtype, name=name, tag=tag or name, align_bytes=64)

        offs_sb = keep.tile([P, S // PER_COLUMN], U16, name="offs_sb")
        tau_sb = keep.tile([P, S // PER_COLUMN], U16, name="tau_sb")
        whose_sb = keep.tile([P, S // PER_COLUMN], U16, name="whose_sb")
        xs_all = sb([P, T], U8, "xs_all")
        es_all = sb([P, T], U8, "es_all")
        xw_all = sb([P, T], I32, "xw_all")
        ew_all = sb([P, T], I32, "ew_all")

        warm_in = sb([P, 1], F32, "warm_in")
        warm_out = sb([P, 1], F32, "warm_out")
        nc.vector.memset(warm_in[:], 0.0)
        nc.scalar.activation(warm_out[:], warm_in[:], ACT.Relu)

        def load_scales(dst, src):
            for q in range(P // QUADRANT):
                rows = src[0, 4 * q : 4 * q + 4, :].bitcast(I32)
                nc.sync.dma_start(
                    out=dst[QUADRANT * q : QUADRANT * (q + 1), :].bitcast(I32),
                    in_=rows.unsqueeze(0).to_broadcast([QUADRANT // 4, 4, T // 4]),
                )

        def load_words(dst, src):
            nc.sync.dma_start(out=dst[:], in_=src[0].rearrange("p n t -> p (n t)").bitcast(I32))

        def load_weight_half(w, c, name):
            raw = sb([P, PACK, H // 2], F32, "%s_raw%d" % (name, c))
            cols = slice(c * (H // 2), (c + 1) * (H // 2))
            nc.sync.dma_start(out=raw[:], in_=w.rearrange("(p j) n -> p j n", j=PACK)[:, :, cols])
            return raw

        nc.sync.dma_start(offs_sb[:], offs)
        load_scales(xs_all, x_scales)
        load_words(xw_all, x_words)
        w1_raw = [load_weight_half(w1, 0, "w1")]
        nc.sync.dma_start(tau_sb[:], tau)
        load_scales(es_all, e_scales)
        w1_raw.append(load_weight_half(w1, 1, "w1"))
        load_words(ew_all, e_words)
        w2_raw = [load_weight_half(w2, 0, "w2")]
        nc.sync.dma_start(whose_sb[:], whose)
        w2_raw.append(load_weight_half(w2, 1, "w2"))
        w3_raw = sb([P, PACK, N], F32, "w3_raw")
        w3_view = w3.rearrange("(g t e) n -> t g e n", t=PACK, e=RUN)
        for t in range(PACK):
            nc.sync.dma_start(out=w3_raw[:, t, :], in_=w3_view[t])
        bias_sb = [sb([P, 1], F32, "bias_sb%d" % t) for t in range(PACK)]
        bias_view = bias.rearrange("(g t e) o -> t g e o", t=PACK, e=RUN)
        with nc.allow_non_contiguous_dma(reason="one float for each partition"):
            for t in range(PACK):
                nc.sync.dma_start(out=bias_sb[t][:], in_=bias_view[t])

        def gather_packed(words_all, scales_all, entries, name):
            words = sb([P, S], U32, name + "_words")
            scales = sb([P, S], U8, name + "_scales")
            nc.vector.tensor_copy(scales[:], scales_all[:].indirect(entries[:]))
            nc.vector.tensor_copy(words[:], words_all[:].bitcast(U32).indirect(entries[:]))
            return words, scales

        def round_half_on_scalar(raw, c, grouped):
            src = raw[:].rearrange("p j (g t e) -> p t g j e", t=PACK, e=RUN)
            for t in range(PACK):
                dst = grouped[t][:, c * (P // 2) : (c + 1) * (P // 2), :].rearrange("p (g e) j -> p g j e", e=RUN)
                nc.scalar.copy(dst, src[:, t])

        def quantize(grouped, width, name):
            codes = sb([P, width], U32, name + "_codes")
            scales = sb([P, width], U8, name + "_scales")
            nc.vector.quantize_mx(
                out=codes[:].bitcast(FP8X4), scales=scales[:], in_=grouped[:].rearrange("p c j -> p (c j)")
            )
            return codes, scales

        def product(acc, stationary, moving):
            nc.tensor.matmul_mx(
                out=acc[:],
                lhsT=stationary[0][:].bitcast(FP8X4),
                lhsT_scale=stationary[1][:],
                rhs=moving[0][:].bitcast(FP8X4),
                rhs_scale=moving[1][:],
                start=True,
                stop=True,
            )

        xq = gather_packed(xw_all, xs_all, offs_sb, "xq")
        w1_grouped = [sb([P, P, PACK], BF16, "w1_grouped%d" % t) for t in range(PACK)]

        picked = [sb([P, PACK * R], F32, "picked%d" % a) for a in range(HALVES)]
        w2_all = picked[1][:].bitcast(BF16).rearrange("p (t c j) -> p t c j", t=PACK, j=PACK)
        w2_grouped = [w2_all[:, t] for t in range(PACK)]

        for c in range(2):
            round_half_on_scalar(w1_raw[c], c, w1_grouped)
        h_acc = []
        for t in range(PACK):
            w1q = quantize(w1_grouped[t], P, "w1q%d" % t)
            acc = psum.tile([P, S], F32, name="h_acc%d" % t, tag="bank%d" % t)
            product(acc, w1q, xq)
            h_acc.append(acc)
        nc.vector.tensor_copy(
            w2_all[:, :, 0 : P // 2, :].rearrange("p t (g e) j -> p g t j e", e=RUN),
            w2_raw[0][:].rearrange("p j (g t e) -> p g t j e", t=PACK, e=RUN),
        )
        eq = gather_packed(ew_all, es_all, tau_sb, "eq")

        h = [sb([P, S], F32, "h%d" % t) for t in range(PACK)]

        def pick(a, t):
            entries = whose_sb[:, a * (R // PER_COLUMN) : (a + 1) * (R // PER_COLUMN)]
            nc.vector.tensor_copy(picked[a][:, t * R : (t + 1) * R], h[t][:].indirect(entries))

        for t in range(PACK):
            nc.scalar.activation(h[t][:], h_acc[t][:], ACT.Relu)
            pick(0, t)

        round_half_on_scalar(w2_raw[1], 1, w2_grouped)
        phi = sb([P, PACK, S], F32, "phi")
        for t in range(PACK):
            w2q = quantize(w2_grouped[t], P, "w2q%d" % t)
            acc = psum.tile([P, S], F32, name="phi_acc%d" % t, tag="bank%d" % (PACK + t))
            product(acc, w2q, eq)
            step = R if t == PACK - 1 else S
            for c0 in range(0, S, step):
                nc.scalar.activation(phi[:, t, c0 : c0 + step], acc[:, c0 : c0 + step], ACT.Relu, bias=bias_sb[t][:])
        for t in range(PACK):
            pick(1, t)

        w3_grouped = sb([P, N, PACK], BF16, "w3_grouped", tag="bias_sb%d" % (PACK - 1))
        nc.scalar.activation(
            w3_grouped[:].rearrange("p (c e) t -> p c t e", e=RUN),
            w3_raw[:].rearrange("p t (c e) -> p c t e", e=RUN),
            ACT.Copy,
            scale=1.0 / D,
        )
        w3q = quantize(w3_grouped, N, "w3q")

        z = [sb([P, R, PACK], BF16, "z%d" % a) for a in range(HALVES)]
        for a in range(HALVES):
            nc.vector.tensor_tensor(
                z[a][:].rearrange("p (c e) t -> p c t e", e=RUN),
                picked[a][:].rearrange("p (t c e) -> p c t e", t=PACK, e=RUN),
                phi[:, :, a * R : (a + 1) * R].rearrange("p t (c e) -> p c t e", e=RUN),
                ALU.mult,
            )
        qv_scaled = []
        for a in range(HALVES):
            zq = quantize(z[a], R, "zq%d" % a)
            acc = psum.tile([P, R], F32, name="qv%d" % a, tag="bank%d" % a)
            product(acc, w3q, zq)
            qv_scaled.append(acc[:].rearrange("p (v d) -> p v d", d=D))

        mq = [sb([P, V], F32, "mq%d" % a) for a in range(HALVES)]
        dev = [sb([P, V, D], F32, "dev%d" % a) for a in range(HALVES)]
        result = sb([P, HALVES * V], F32, "result")
        for a in range(HALVES):
            nc.vector.tensor_reduce(mq[a][:], qv_scaled[a], AXIS.X, ALU.add)
        for a in range(HALVES):
            nc.vector.scalar_tensor_tensor(
                dev[a][:], mq[a][:].unsqueeze(2).to_broadcast([P, V, D]), -1.0 / D, qv_scaled[a], ALU.mult, ALU.add
            )
        for a in range(HALVES):
            nc.vector.tensor_reduce(
                result[:, a * V : (a + 1) * V], dev[a][:], AXIS.X, ALU.add, apply_absolute_value=True
            )
        nc.sync.dma_start(out=out, in_=result[:])
